import numpy as np
import ml_dtypes


def mxq(x, axis, fmt="e4m3"):
    dtype, down = {"e4m3": (ml_dtypes.float8_e4m3fn, 7), "e5m2": (ml_dtypes.float8_e5m2, 14)}[fmt]
    v = np.moveaxis(np.asarray(x, np.float32).astype(ml_dtypes.bfloat16).astype(np.float64), axis, -1)
    blocks = v.reshape(v.shape[:-1] + (-1, 32))
    amax = np.abs(blocks).max(-1, keepdims=True)
    byte = np.maximum(np.where(amax > 0, np.frexp(amax)[1] - 1 + 127, 0) - down, 1)
    scale = np.exp2(byte - 127.0)
    codes = (blocks / scale).astype(np.float32).astype(dtype).astype(np.float64)
    return np.moveaxis((codes * scale).reshape(v.shape), -1, axis)


WIDE = False


def mx_kscale(k):
    if not WIDE:
        return np.ones(k)
    levels = np.array([10, -10, 5, -5, 0])
    if k % 512:
        return np.exp2(np.random.permutation(np.resize(levels, k // 32))).repeat(32)
    a = np.empty((k // 512, 16))
    for p in range(k // 512):
        a[p, :8] = np.random.permutation(np.resize(levels, 8))
        for g in range(8):
            far = levels[np.abs(levels - a[p, g]) >= 10]
            a[p, g + 8] = far[np.random.randint(len(far))]
    return np.exp2(a.ravel()).repeat(32)


def f64(x):
    return np.asarray(x).astype(np.float64)


def striped(idx):
    return np.tile(idx.reshape(-1, 16).T, (8, 1)).astype(np.uint16)


def unstriped(offs):
    return offs[:16].T.reshape(-1).astype(np.int64)


def pack_weight(w):
    k, n = w.shape
    w = f64(np.asarray(w, np.float32).astype(ml_dtypes.bfloat16)).reshape(k // 32, 32, n)
    amax = np.abs(w).max(1)
    byte = np.clip(np.where(amax > 0, np.frexp(amax)[1] - 1 + 127 - 7, 1), 1, 254)
    scaled = (w * np.exp2(127.0 - byte)[:, None, :]).reshape(k, n).astype(np.float32)
    words = np.ascontiguousarray(scaled.reshape(k // 512, 128, 4, n).transpose(0, 1, 3, 2)).astype(ml_dtypes.float8_e4m3fn).view(np.uint8)
    return words, np.ascontiguousarray(byte.astype(np.uint8).reshape(k // 512, 16, n))


def unpack_weight(words, scales):
    g, p, n, _ = words.shape
    vals = np.ascontiguousarray(words).view(ml_dtypes.float8_e4m3fn).astype(np.float64) * np.repeat(np.exp2(scales.astype(np.float64) - 127.0), 8, axis=1)[..., None]
    return vals.transpose(0, 1, 3, 2).reshape(g * 512, n)


K, T, S, N = 1024, 1024, 512, 256
P = 2 ** 7


def setup_inputs():
    n = np.random.standard_normal
    s = mx_kscale(K)[:, None]
    packed_xT = pack_weight(n((K, T)) * s)
    return {
        "x_words": packed_xT[0],
        "x_scales": packed_xT[1],
        "w1": (n((K, N)) / np.sqrt(K) / s).astype(np.float32),
        "w2": (n((K, N)) / np.sqrt(K) / s).astype(np.float32),
        "w3": (n((K, N)) / np.sqrt(K) / s).astype(np.float32),
        "buys": (np.tile((np.random.uniform(size=S) < 0.5) * 1.0, (P, 1))).astype(np.float32),
        "logv": (n((N, S))).astype(np.float32),
        "offs": striped(np.random.permutation(T)[:S]),
    }


def reference(x_words, x_scales, w1, w2, w3, buys, logv, offs):
    xq = unpack_weight(x_words, x_scales)[:, unstriped(offs)]
    yp = mxq(f64(w1), 0, "e4m3").T @ xq
    ys = mxq(f64(w3), 0, "e4m3").T @ xq
    sg = 0.7 * (np.log(np.exp(ys) + 1.0)) + 0.3
    ym = mxq(f64(w2), 0, "e4m3").T @ xq
    return np.log(np.exp(yp) + 1.0) - (f64(buys)[:1] * yp) + f64(buys)[:1] * (np.log(sg) + 0.5 * (((f64(logv) - ym) / sg) ** 2))

@@ -1,0 +1,202 @@
+import math
+from contextlib import ExitStack
+
+import concourse.mybir as mybir
+from concourse.masks import make_identity
+
+K, T, S, N = 1024, 1024, 512, 256
+FLOPS = 3 * 2 * K * S * N
+
+F32 = mybir.dt.float32
+BF16 = mybir.dt.bfloat16
+I32 = mybir.dt.int32
+U32 = mybir.dt.uint32
+U16 = mybir.dt.uint16
+U8 = mybir.dt.uint8
+FP8X4 = mybir.dt.float8_e4m3fn_x4
+ALU = mybir.AluOpType
+ACT = mybir.ActivationFunctionType
+
+P = 128
+PACK = 4
+PASSES = K // (P * PACK)
+JT = S // P
+MT = N // P
+SHIFT = 0.3 / 0.7
+FLOOR = 2.0 ** -63
+
+
+def tile_picked_yziln_nll_p_kernel(tc, x_words, x_scales, w1, w2, w3, buys, logv, offs, out):
+    nc = tc.nc
+    with ExitStack() as ctx:
+        keep = ctx.enter_context(tc.tile_pool(name="keep", bufs=1))
+        psum = ctx.enter_context(tc.psum_pool(name="psum", bufs=1))
+
+        offsets = keep.tile([P, S // 16], U16, name="offsets")
+        scale_table = keep.tile([P, T], U8, name="scale_table", align_bytes=64)
+        warm = keep.tile([P, 1], F32, name="warm")
+        warm_out = keep.tile([P, 1], F32, name="warm_out")
+        nc.vector.memset(scale_table[:].bitcast(I32), 0)
+        nc.vector.memset(warm[:], 0.0)
+        nc.scalar.activation(warm_out[:], warm[:], ACT.Sigmoid)
+
+        nc.sync.dma_start(offsets[:], offs)
+        word_tables = [keep.tile([P, T], U32, name=f"word_table{o}", align_bytes=64) for o in range(PASSES)]
+
+        def load_words(o):
+            nc.sync.dma_start(word_tables[o][:].bitcast(I32), x_words[o].rearrange("p n t -> p (n t)").bitcast(I32))
+
+        for q in range(4):
+            nc.sync.dma_start(scale_table[32 * q:32 * q + 8, :].bitcast(I32), x_scales[:, 4 * q:4 * q + 4, :].bitcast(I32))
+        load_words(0)
+        load_words(1)
+
+        raw = {}
+
+        def load_weights(name, w):
+            for o in range(PASSES):
+                raw[name, o] = keep.tile([P, PACK, N], F32, name=f"raw_{name}{o}")
+                nc.sync.dma_start(raw[name, o][:], w[512 * o:512 * (o + 1), :].rearrange("(p t) m -> p t m", t=PACK))
+
+        load_weights("s", w3)
+        load_weights("p", w1)
+        load_weights("m", w2)
+        spent = keep.tile([P, MT, S], F32, name="spent")
+        nc.sync.dma_start(spent[:], logv.rearrange("(t p) j -> p t j", p=P))
+        bought = keep.tile([P, JT], F32, name="bought")
+        with nc.allow_non_contiguous_dma(reason="one flag a partition"):
+            nc.sync.dma_start(bought[:], buys[0].rearrange("(t p) -> p t", p=P))
+
+        identity = keep.tile([P, P], F32, name="identity")
+        make_identity(nc, identity[:])
+
+        x_planes = keep.tile([P, S], U8, name="x_planes", align_bytes=64)
+        x_codes = [keep.tile([P, S], U32, name=f"x_codes{o}", align_bytes=64) for o in range(PASSES)]
+        nc.vector.tensor_copy(x_planes[:], scale_table[:].indirect(offsets[:]))
+        nc.vector.tensor_copy(x_codes[0][:], word_tables[0][:].indirect(offsets[:]))
+        nc.vector.tensor_copy(x_codes[1][:], word_tables[1][:].indirect(offsets[:]))
+
+        codes, planes = {}, {}
+
+        def quantise(name, o, sign, on_scalar=False):
+            grouped = keep.tile([P, N, PACK], BF16, name=f"grouped_{name}{o}", align_bytes=64)
+            dst = grouped[:].rearrange("p (c i) t -> p c t i", i=4)
+            src = raw[name, o][:].rearrange("p t (c i) -> p c t i", i=4)
+            if on_scalar:
+                nc.scalar.activation(dst, src, ACT.Copy, scale=sign)
+            else:
+                nc.vector.tensor_scalar(dst, src, sign, None, ALU.mult)
+            codes[name, o] = keep.tile([P, N], U32, name=f"codes_{name}{o}", align_bytes=64)
+            planes[name, o] = keep.tile([P, N], U8, name=f"plane_{name}{o}", align_bytes=64)
+            nc.vector.quantize_mx(out=codes[name, o][:].bitcast(FP8X4), scales=planes[name, o][:], in_=grouped[:].rearrange("p m t -> p (m t)"))
+
+        def product_by_customer(dst, name, jt, o):
+            cols = slice(jt * P, (jt + 1) * P)
+            nc.tensor.matmul_mx(out=dst, lhsT=x_codes[o][:, cols].bitcast(FP8X4), lhsT_scale=x_planes[4 * o:P, cols],
+                                rhs=codes[name, o][:].bitcast(FP8X4), rhs_scale=planes[name, o][:],
+                                start=(o == 0), stop=(o == PASSES - 1))
+
+        sig = keep.tile([P, JT, 2 * N], F32, name="sig")
+        share = N // JT
+
+        def s_part(tile, jt):
+            return tile[:, jt, 0:N]
+
+        def p_part(tile, jt):
+            return tile[:, :, N + jt * share:N + (jt + 1) * share]
+
+        def in_shares(ap):
+            return ap.rearrange("p (c i) -> p c i", i=share)
+
+        quantise("s", 0, -1.0, on_scalar=True)
+        quantise("s", 1, -1.0)
+        neg_s = [psum.tile([P, 2, N], F32, name=f"neg_s{h}", tag=f"s{h}") for h in range(2)]
+        for jt in range(JT):
+            for o in range(PASSES):
+                product_by_customer(neg_s[jt // 2][:, jt % 2, :], "s", jt, o)
+            if jt % 2 == 1:
+                nc.scalar.activation(sig[:, jt - 1:jt + 1, 0:N], neg_s[jt // 2][:], ACT.Sigmoid)
+
+        neg_p = [psum.tile([P, N], F32, name=f"neg_p{jt}", tag=f"p{jt}") for jt in range(JT)]
+        for o in range(PASSES):
+            quantise("p", o, -1.0)
+            for jt in range(JT):
+                product_by_customer(neg_p[jt][:], "p", jt, o)
+        for jt in range(JT):
+            nc.scalar.activation(p_part(sig, jt), in_shares(neg_p[jt][:]), ACT.Sigmoid)
+
+        mean = [psum.tile([P, S], F32, name=f"mean{mt}", tag=f"m{mt}") for mt in range(MT)]
+        for o in range(PASSES):
+            quantise("m", o, 1.0)
+            for mt in range(MT):
+                cols = slice(mt * P, (mt + 1) * P)
+                nc.tensor.matmul_mx(out=mean[mt][:], lhsT=codes["m", o][:, cols].bitcast(FP8X4), lhsT_scale=planes["m", o][:, cols],
+                                    rhs=x_codes[o][:].bitcast(FP8X4), rhs_scale=x_planes[4 * o:P, :],
+                                    start=(o == 0), stop=(o == PASSES - 1))
+
+        sg_scale = keep.tile([P, JT], F32, name="sg_scale")
+        sg_bias = keep.tile([P, JT], F32, name="sg_bias")
+        half_bought = keep.tile([P, JT], F32, name="half_bought")
+        nc.gpsimd.tensor_scalar(sg_scale[:], bought[:], -0.7, 0.0, ALU.mult, ALU.add)
+        nc.gpsimd.tensor_scalar(sg_bias[:], bought[:], -1.0, 1.0, ALU.mult, ALU.add)
+        nc.gpsimd.tensor_scalar(half_bought[:], bought[:], 0.5, 0.0, ALU.mult, ALU.add)
+
+        miss = keep.tile([P, MT, S], F32, name="miss")
+        miss_sq = keep.tile([P, MT, S], F32, name="miss_sq")
+        for mt in range(MT):
+            nc.vector.tensor_tensor(miss[:, mt, :], mean[mt][:], spent[:, mt, :], ALU.subtract)
+
+        logsig = keep.tile([P, JT, 2 * N], F32, name="logsig")
+        soft = keep.tile([P, 2, JT, N], F32, name="soft")
+        for jt in range(JT):
+            nc.scalar.activation(logsig[:, jt, :], sig[:, jt, :], ACT.Ln, bias=FLOOR, scale=math.exp(-SHIFT))
+            nc.vector.scalar_tensor_tensor(soft[:, 0, jt, :], neg_s[jt // 2][:, jt % 2, :], SHIFT, s_part(logsig, jt), ALU.subtract, ALU.min)
+
+        log_sg = keep.tile([P, JT, N], F32, name="log_sg")
+        for jt in range(JT):
+            nc.scalar.activation(log_sg[:, jt, :], soft[:, 0, jt, :], ACT.Ln, bias=sg_bias[:, jt:jt + 1], scale=sg_scale[:, jt:jt + 1])
+
+        for mt in range(MT):
+            nc.vector.tensor_tensor(miss_sq[:, mt, :], miss[:, mt, :], miss[:, mt, :], ALU.mult)
+        miss_sq_t = [psum.tile([P, JT, P], F32, name=f"miss_sq_t{mt}", tag=f"m{mt}") for mt in range(MT)]
+        for mt in range(MT):
+            for jt in range(JT):
+                nc.tensor.transpose(miss_sq_t[mt][:, jt, :], miss_sq[:, mt, jt * P:(jt + 1) * P], identity[:])
+
+        odds = keep.tile([P, JT, N], F32, name="odds")
+        for jt in range(JT):
+            nc.vector.scalar_tensor_tensor(in_shares(soft[:, 1, jt, :]), in_shares(neg_p[jt][:]), SHIFT, p_part(logsig, jt), ALU.subtract, ALU.min)
+        for jt in range(JT):
+            nc.vector.scalar_tensor_tensor(odds[:, jt, :], neg_p[jt][:], bought[:, jt:jt + 1], soft[:, 1, jt, :], ALU.mult, ALU.subtract)
+
+        total = [[psum.tile([P, 2, P], F32, name=f"total{h}{mt}", tag=f"p{2 * h + mt}") for mt in range(MT)] for h in range(2)]
+
+        def add_turned(term, jt, mt, first, last):
+            nc.tensor.matmul(total[jt // 2][mt][:, jt % 2, :], term[:, jt, mt * P:(mt + 1) * P], identity[:],
+                             is_transpose=True, start=first and jt % 2 == 0, stop=last and jt % 2 == 1)
+
+        for term in (log_sg, odds):
+            for jt in range(JT):
+                for mt in range(MT):
+                    add_turned(term, jt, mt, term is log_sg, False)
+
+        inv_var = keep.tile([P, JT, N], F32, name="inv_var")
+        fit = keep.tile([P, JT, N], F32, name="fit")
+        for mt in range(MT):
+            cols = slice(mt * P, (mt + 1) * P)
+            nc.scalar.activation(inv_var[:, :, cols], log_sg[:, :, cols], ACT.Exp, scale=-2.0)
+        for mt in range(MT):
+            cols = slice(mt * P, (mt + 1) * P)
+            for jt in range(JT):
+                nc.vector.scalar_tensor_tensor(fit[:, jt, cols], miss_sq_t[mt][:, jt, :], half_bought[:, jt:jt + 1], inv_var[:, jt, cols], ALU.mult, ALU.mult)
+                add_turned(fit, jt, mt, False, True)
+        for mt in range(MT):
+            result = keep.tile([P, S], F32, name=f"result{mt}")
+            for h in range(2):
+                dst = result[:, h * 2 * P:(h + 1) * 2 * P]
+                src = total[h][mt][:].rearrange("p a b -> p (a b)")
+                if mt == 1 and h == 1:
+                    nc.vector.tensor_scalar(dst, src, SHIFT, None, ALU.subtract)
+                else:
+                    nc.scalar.activation(dst, src, ACT.Copy, bias=-SHIFT)
+            nc.sync.dma_start(out[mt * P:(mt + 1) * P, :], result[:])

@@ -36,31 +36,30 @@ def tile_picked_yziln_nll_p_kernel(tc, x_words, x_scales, w1, w2, w3, buys, logv
         scale_table = keep.tile([P, T], U8, name="scale_table", align_bytes=64)
         warm = keep.tile([P, 1], F32, name="warm")
         warm_out = keep.tile([P, 1], F32, name="warm_out")
-        nc.vector.memset(scale_table[:].bitcast(I32), 0)
-        nc.vector.memset(warm[:], 0.0)
-        nc.scalar.activation(warm_out[:], warm[:], ACT.Sigmoid)
-
-        nc.sync.dma_start(offsets[:], offs)
+        nc.gpsimd.memset(scale_table[:].bitcast(I32), 0)
+        nc.gpsimd.memset(warm[:], 0.0)
         word_tables = [keep.tile([P, T], U32, name=f"word_table{o}", align_bytes=64) for o in range(PASSES)]
 
         def load_words(o):
             nc.sync.dma_start(word_tables[o][:].bitcast(I32), x_words[o].rearrange("p n t -> p (n t)").bitcast(I32))
 
+        load_words(0)
+        nc.sync.dma_start(offsets[:], offs)
         for q in range(4):
             nc.sync.dma_start(scale_table[32 * q:32 * q + 8, :].bitcast(I32), x_scales[:, 4 * q:4 * q + 4, :].bitcast(I32))
-        load_words(0)
-        load_words(1)
-
+        nc.scalar.activation(warm_out[:], warm[:], ACT.Sigmoid)
         raw = {}
 
-        def load_weights(name, w):
-            for o in range(PASSES):
-                raw[name, o] = keep.tile([P, PACK, N], F32, name=f"raw_{name}{o}")
-                nc.sync.dma_start(raw[name, o][:], w[512 * o:512 * (o + 1), :].rearrange("(p t) m -> p t m", t=PACK))
+        def load_weights(name, w, o):
+            raw[name, o] = keep.tile([P, PACK, N], F32, name=f"raw_{name}{o}")
+            nc.sync.dma_start(raw[name, o][:], w[512 * o:512 * (o + 1), :].rearrange("(p t) m -> p t m", t=PACK))
 
-        load_weights("s", w3)
-        load_weights("p", w1)
-        load_weights("m", w2)
+        load_weights("s", w3, 0)
+        load_words(1)
+        load_weights("s", w3, 1)
+        for name, w in (("p", w1), ("m", w2)):
+            for o in range(PASSES):
+                load_weights(name, w, o)
         spent = keep.tile([P, MT, S], F32, name="spent")
         nc.sync.dma_start(spent[:], logv.rearrange("(t p) j -> p t j", p=P))
         bought = keep.tile([P, JT], F32, name="bought")
@@ -72,8 +71,8 @@ def tile_picked_yziln_nll_p_kernel(tc, x_words, x_scales, w1, w2, w3, buys, logv
 
         x_planes = keep.tile([P, S], U8, name="x_planes", align_bytes=64)
         x_codes = [keep.tile([P, S], U32, name=f"x_codes{o}", align_bytes=64) for o in range(PASSES)]
-        nc.vector.tensor_copy(x_planes[:], scale_table[:].indirect(offsets[:]))
         nc.vector.tensor_copy(x_codes[0][:], word_tables[0][:].indirect(offsets[:]))
+        nc.vector.tensor_copy(x_planes[:], scale_table[:].indirect(offsets[:]))
         nc.vector.tensor_copy(x_codes[1][:], word_tables[1][:].indirect(offsets[:]))
 
         codes, planes = {}, {}
@@ -99,31 +98,27 @@ def tile_picked_yziln_nll_p_kernel(tc, x_words, x_scales, w1, w2, w3, buys, logv
         sig = keep.tile([P, JT, 2 * N], F32, name="sig")
         share = N // JT
 
-        def s_part(tile, jt):
-            return tile[:, jt, 0:N]
-
         def p_part(tile, jt):
-            return tile[:, :, N + jt * share:N + (jt + 1) * share]
+            return tile[:, :, N + (JT - 1 - jt) * share:N + (JT - jt) * share]
 
         def in_shares(ap):
             return ap.rearrange("p (c i) -> p c i", i=share)
 
-        quantise("s", 0, -1.0, on_scalar=True)
-        quantise("s", 1, -1.0)
-        neg_s = [psum.tile([P, 2, N], F32, name=f"neg_s{h}", tag=f"s{h}") for h in range(2)]
+        banks = [psum.tile([P, 2, N], F32, name=f"neg{b}", tag=f"b{b}") for b in range(6)]
+        neg_s = [banks[jt][:, 0, :] for jt in range(JT)]
+        neg_p = [banks[4][:, 0, :], banks[5][:, 0, :], banks[0][:, 1, :], banks[1][:, 1, :]]
+        for o in range(PASSES):
+            quantise("s", o, -1.0, on_scalar=True)
+            for jt in range(JT):
+                product_by_customer(neg_s[jt], "s", jt, o)
         for jt in range(JT):
-            for o in range(PASSES):
-                product_by_customer(neg_s[jt // 2][:, jt % 2, :], "s", jt, o)
-            if jt % 2 == 1:
-                nc.scalar.activation(sig[:, jt - 1:jt + 1, 0:N], neg_s[jt // 2][:], ACT.Sigmoid)
-
-        neg_p = [psum.tile([P, N], F32, name=f"neg_p{jt}", tag=f"p{jt}") for jt in range(JT)]
+            nc.scalar.activation(sig[:, jt, 0:N], neg_s[jt], ACT.Sigmoid)
         for o in range(PASSES):
             quantise("p", o, -1.0)
             for jt in range(JT):
-                product_by_customer(neg_p[jt][:], "p", jt, o)
+                product_by_customer(neg_p[jt], "p", jt, o)
         for jt in range(JT):
-            nc.scalar.activation(p_part(sig, jt), in_shares(neg_p[jt][:]), ACT.Sigmoid)
+            nc.scalar.activation(p_part(sig, jt), in_shares(neg_p[jt]), ACT.Sigmoid)
 
         mean = [psum.tile([P, S], F32, name=f"mean{mt}", tag=f"m{mt}") for mt in range(MT)]
         for o in range(PASSES):
@@ -136,10 +131,8 @@ def tile_picked_yziln_nll_p_kernel(tc, x_words, x_scales, w1, w2, w3, buys, logv
 
         sg_scale = keep.tile([P, JT], F32, name="sg_scale")
         sg_bias = keep.tile([P, JT], F32, name="sg_bias")
-        half_bought = keep.tile([P, JT], F32, name="half_bought")
         nc.gpsimd.tensor_scalar(sg_scale[:], bought[:], -0.7, 0.0, ALU.mult, ALU.add)
         nc.gpsimd.tensor_scalar(sg_bias[:], bought[:], -1.0, 1.0, ALU.mult, ALU.add)
-        nc.gpsimd.tensor_scalar(half_bought[:], bought[:], 0.5, 0.0, ALU.mult, ALU.add)
 
         miss = keep.tile([P, MT, S], F32, name="miss")
         miss_sq = keep.tile([P, MT, S], F32, name="miss_sq")
@@ -148,28 +141,32 @@ def tile_picked_yziln_nll_p_kernel(tc, x_words, x_scales, w1, w2, w3, buys, logv
 
         logsig = keep.tile([P, JT, 2 * N], F32, name="logsig")
         soft = keep.tile([P, 2, JT, N], F32, name="soft")
-        for jt in range(JT):
-            nc.scalar.activation(logsig[:, jt, :], sig[:, jt, :], ACT.Ln, bias=FLOOR, scale=math.exp(-SHIFT))
-            nc.vector.scalar_tensor_tensor(soft[:, 0, jt, :], neg_s[jt // 2][:, jt % 2, :], SHIFT, s_part(logsig, jt), ALU.subtract, ALU.min)
+        cut = N + share // 2
+        for h in range(2):
+            rows = slice(2 * h, 2 * h + 2)
+            nc.scalar.activation(logsig[:, rows, 0:cut], sig[:, rows, 0:cut], ACT.Ln, bias=FLOOR, scale=math.exp(-SHIFT))
+            for jt in range(2 * h, 2 * h + 2):
+                nc.vector.scalar_tensor_tensor(soft[:, 0, jt, :], neg_s[jt], SHIFT, logsig[:, jt, 0:N], ALU.subtract, ALU.min)
+        nc.scalar.activation(logsig[:, :, cut:2 * N], sig[:, :, cut:2 * N], ACT.Ln, bias=FLOOR, scale=math.exp(-SHIFT))
 
         log_sg = keep.tile([P, JT, N], F32, name="log_sg")
         for jt in range(JT):
             nc.scalar.activation(log_sg[:, jt, :], soft[:, 0, jt, :], ACT.Ln, bias=sg_bias[:, jt:jt + 1], scale=sg_scale[:, jt:jt + 1])
 
         for mt in range(MT):
-            nc.vector.tensor_tensor(miss_sq[:, mt, :], miss[:, mt, :], miss[:, mt, :], ALU.mult)
-        miss_sq_t = [psum.tile([P, JT, P], F32, name=f"miss_sq_t{mt}", tag=f"m{mt}") for mt in range(MT)]
-        for mt in range(MT):
-            for jt in range(JT):
-                nc.tensor.transpose(miss_sq_t[mt][:, jt, :], miss_sq[:, mt, jt * P:(jt + 1) * P], identity[:])
+            nc.gpsimd.tensor_tensor(miss_sq[:, mt, :], miss[:, mt, :], miss[:, mt, :], ALU.mult)
+        miss_sq_t = [psum.tile([P, 2, N], F32, name=f"miss_sq_t{h}", tag=f"m{h}") for h in range(2)]
+        for jt in range(JT):
+            for mt in range(MT):
+                nc.tensor.transpose(miss_sq_t[jt // 2][:, jt % 2, mt * P:(mt + 1) * P], miss_sq[:, mt, jt * P:(jt + 1) * P], identity[:])
 
         odds = keep.tile([P, JT, N], F32, name="odds")
         for jt in range(JT):
-            nc.vector.scalar_tensor_tensor(in_shares(soft[:, 1, jt, :]), in_shares(neg_p[jt][:]), SHIFT, p_part(logsig, jt), ALU.subtract, ALU.min)
+            nc.vector.scalar_tensor_tensor(in_shares(soft[:, 1, jt, :]), in_shares(neg_p[jt]), SHIFT, p_part(logsig, jt), ALU.subtract, ALU.min)
         for jt in range(JT):
-            nc.vector.scalar_tensor_tensor(odds[:, jt, :], neg_p[jt][:], bought[:, jt:jt + 1], soft[:, 1, jt, :], ALU.mult, ALU.subtract)
+            nc.vector.scalar_tensor_tensor(odds[:, jt, :], neg_p[jt], bought[:, jt:jt + 1], soft[:, 1, jt, :], ALU.mult, ALU.subtract)
 
-        total = [[psum.tile([P, 2, P], F32, name=f"total{h}{mt}", tag=f"p{2 * h + mt}") for mt in range(MT)] for h in range(2)]
+        total = [[psum.tile([P, 2, P], F32, name=f"total{h}{mt}", tag=f"b{2 + 2 * h + mt}") for mt in range(MT)] for h in range(2)]
 
         def add_turned(term, jt, mt, first, last):
             nc.tensor.matmul(total[jt // 2][mt][:, jt % 2, :], term[:, jt, mt * P:(mt + 1) * P], identity[:],
@@ -182,21 +179,21 @@ def tile_picked_yziln_nll_p_kernel(tc, x_words, x_scales, w1, w2, w3, buys, logv
 
         inv_var = keep.tile([P, JT, N], F32, name="inv_var")
         fit = keep.tile([P, JT, N], F32, name="fit")
-        for mt in range(MT):
-            cols = slice(mt * P, (mt + 1) * P)
-            nc.scalar.activation(inv_var[:, :, cols], log_sg[:, :, cols], ACT.Exp, scale=-2.0)
-        for mt in range(MT):
-            cols = slice(mt * P, (mt + 1) * P)
-            for jt in range(JT):
-                nc.vector.scalar_tensor_tensor(fit[:, jt, cols], miss_sq_t[mt][:, jt, :], half_bought[:, jt:jt + 1], inv_var[:, jt, cols], ALU.mult, ALU.mult)
+        fit_bias = keep.tile([P, JT], F32, name="fit_bias")
+        nc.gpsimd.tensor_scalar(fit_bias[:], sg_bias[:], -200.0, math.log(0.5), ALU.mult, ALU.add)
+        for jt in range(JT):
+            nc.scalar.activation(inv_var[:, jt, :], log_sg[:, jt, :], ACT.Exp, scale=-2.0, bias=fit_bias[:, jt:jt + 1])
+        for jt in range(JT):
+            nc.vector.tensor_tensor(fit[:, jt, :], miss_sq_t[jt // 2][:, jt % 2, :], inv_var[:, jt, :], ALU.mult)
+            for mt in range(MT):
                 add_turned(fit, jt, mt, False, True)
+        out_view = out.rearrange("(t p) j -> p t j", p=P)
+        early = keep.tile([P, MT, 2 * P], F32, name="early")
         for mt in range(MT):
-            result = keep.tile([P, S], F32, name=f"result{mt}")
-            for h in range(2):
-                dst = result[:, h * 2 * P:(h + 1) * 2 * P]
-                src = total[h][mt][:].rearrange("p a b -> p (a b)")
-                if mt == 1 and h == 1:
-                    nc.vector.tensor_scalar(dst, src, SHIFT, None, ALU.subtract)
-                else:
-                    nc.scalar.activation(dst, src, ACT.Copy, bias=-SHIFT)
-            nc.sync.dma_start(out[mt * P:(mt + 1) * P, :], result[:])
+            nc.scalar.activation(early[:, mt, :], total[0][mt][:].rearrange("p a b -> p (a b)"), ACT.Copy, bias=-SHIFT)
+        nc.sync.dma_start(out_view[:, :, 0:2 * P], early[:])
+        late = [keep.tile([P, 2 * P], F32, name=f"late{mt}") for mt in range(MT)]
+        nc.scalar.activation(late[0][:], total[1][0][:].rearrange("p a b -> p (a b)"), ACT.Copy, bias=-SHIFT)
+        nc.scalar.dma_start(out_view[:, 0, 2 * P:S], late[0][:])
+        nc.vector.tensor_scalar(late[1][:], total[1][1][:].rearrange("p a b -> p (a b)"), SHIFT, None, ALU.subtract)
+        nc.sync.dma_start(out_view[:, 1, 2 * P:S], late[1][:])

@@ -1,4 +1,3 @@
-import math
 from contextlib import ExitStack
 
 import concourse.mybir as mybir
@@ -22,7 +21,6 @@ PACK = 4
 PASSES = K // (P * PACK)
 JT = S // P
 MT = N // P
-SHIFT = 0.3 / 0.7
 FLOOR = 2.0 ** -63
 
 
@@ -38,6 +36,8 @@ def tile_picked_yziln_nll_p_kernel(tc, x_words, x_scales, w1, w2, w3, buys, logv
         warm_out = keep.tile([P, 1], F32, name="warm_out")
         nc.gpsimd.memset(scale_table[:].bitcast(I32), 0)
         nc.gpsimd.memset(warm[:], 0.0)
+        flag_rows = keep.tile([P, P], F32, name="flag_rows")
+        nc.gpsimd.memset(flag_rows[:], 0.0)
         word_tables = [keep.tile([P, T], U32, name=f"word_table{o}", align_bytes=64) for o in range(PASSES)]
 
         def load_words(o):
@@ -47,6 +47,7 @@ def tile_picked_yziln_nll_p_kernel(tc, x_words, x_scales, w1, w2, w3, buys, logv
         nc.sync.dma_start(offsets[:], offs)
         for q in range(4):
             nc.sync.dma_start(scale_table[32 * q:32 * q + 8, :].bitcast(I32), x_scales[:, 4 * q:4 * q + 4, :].bitcast(I32))
+        nc.gpsimd.dma_start(flag_rows[0:JT, :], buys[0].rearrange("(t p) -> t p", p=P))
         nc.scalar.activation(warm_out[:], warm[:], ACT.Sigmoid)
         raw = {}
 
@@ -62,12 +63,21 @@ def tile_picked_yziln_nll_p_kernel(tc, x_words, x_scales, w1, w2, w3, buys, logv
                 load_weights(name, w, o)
         spent = keep.tile([P, MT, S], F32, name="spent")
         nc.sync.dma_start(spent[:], logv.rearrange("(t p) j -> p t j", p=P))
-        bought = keep.tile([P, JT], F32, name="bought")
-        with nc.allow_non_contiguous_dma(reason="one flag a partition"):
-            nc.sync.dma_start(bought[:], buys[0].rearrange("(t p) -> p t", p=P))
 
         identity = keep.tile([P, P], F32, name="identity")
         make_identity(nc, identity[:])
+        bought = keep.tile([P, JT], F32, name="bought")
+        flags_turned = psum.tile([P, P], F32, name="flags_turned", tag="m0")
+        nc.tensor.transpose(flags_turned[:], flag_rows[:], identity[:])
+        nc.scalar.copy(bought[:], flags_turned[:, 0:JT])
+        sg_scale = keep.tile([P, JT], F32, name="sg_scale")
+        sg_bias = keep.tile([P, JT], F32, name="sg_bias")
+        nc.gpsimd.tensor_scalar(sg_scale[:], bought[:], -0.7, 0.0, ALU.mult, ALU.add)
+        nc.gpsimd.tensor_scalar(sg_bias[:], bought[:], -0.7, 1.0, ALU.mult, ALU.add)
+        side = keep.tile([P, JT], F32, name="side")
+        nc.gpsimd.tensor_scalar(side[:], bought[:], -2.0, 1.0, ALU.mult, ALU.add)
+        fit_bias = keep.tile([P, JT], F32, name="fit_bias")
+        nc.gpsimd.tensor_scalar(fit_bias[:], bought[:], -1.0, 200.0, ALU.add, ALU.mult)
 
         x_planes = keep.tile([P, S], U8, name="x_planes", align_bytes=64)
         x_codes = [keep.tile([P, S], U32, name=f"x_codes{o}", align_bytes=64) for o in range(PASSES)]
@@ -75,19 +85,21 @@ def tile_picked_yziln_nll_p_kernel(tc, x_words, x_scales, w1, w2, w3, buys, logv
         nc.vector.tensor_copy(x_planes[:], scale_table[:].indirect(offsets[:]))
         nc.vector.tensor_copy(x_codes[1][:], word_tables[1][:].indirect(offsets[:]))
 
-        codes, planes = {}, {}
+        grouped, codes, planes = {}, {}, {}
 
-        def quantise(name, o, sign, on_scalar=False):
-            grouped = keep.tile([P, N, PACK], BF16, name=f"grouped_{name}{o}", align_bytes=64)
-            dst = grouped[:].rearrange("p (c i) t -> p c t i", i=4)
+        def round_weights(name, o, sign, on_scalar=False):
+            grouped[name, o] = keep.tile([P, N, PACK], BF16, name=f"grouped_{name}{o}", align_bytes=64)
+            dst = grouped[name, o][:].rearrange("p (c i) t -> p c t i", i=4)
             src = raw[name, o][:].rearrange("p t (c i) -> p c t i", i=4)
             if on_scalar:
                 nc.scalar.activation(dst, src, ACT.Copy, scale=sign)
             else:
                 nc.vector.tensor_scalar(dst, src, sign, None, ALU.mult)
+
+        def quantise(name, o):
             codes[name, o] = keep.tile([P, N], U32, name=f"codes_{name}{o}", align_bytes=64)
             planes[name, o] = keep.tile([P, N], U8, name=f"plane_{name}{o}", align_bytes=64)
-            nc.vector.quantize_mx(out=codes[name, o][:].bitcast(FP8X4), scales=planes[name, o][:], in_=grouped[:].rearrange("p m t -> p (m t)"))
+            nc.vector.quantize_mx(out=codes[name, o][:].bitcast(FP8X4), scales=planes[name, o][:], in_=grouped[name, o][:].rearrange("p m t -> p (m t)"))
 
         def product_by_customer(dst, name, jt, o):
             cols = slice(jt * P, (jt + 1) * P)
@@ -108,31 +120,29 @@ def tile_picked_yziln_nll_p_kernel(tc, x_words, x_scales, w1, w2, w3, buys, logv
         neg_s = [banks[jt][:, 0, :] for jt in range(JT)]
         neg_p = [banks[4][:, 0, :], banks[5][:, 0, :], banks[0][:, 1, :], banks[1][:, 1, :]]
         for o in range(PASSES):
-            quantise("s", o, -1.0, on_scalar=True)
+            round_weights("s", o, -1.0, on_scalar=True)
+            quantise("s", o)
             for jt in range(JT):
                 product_by_customer(neg_s[jt], "s", jt, o)
         for jt in range(JT):
             nc.scalar.activation(sig[:, jt, 0:N], neg_s[jt], ACT.Sigmoid)
         for o in range(PASSES):
-            quantise("p", o, -1.0)
+            round_weights("p", o, -1.0)
+            quantise("p", o)
             for jt in range(JT):
                 product_by_customer(neg_p[jt], "p", jt, o)
         for jt in range(JT):
-            nc.scalar.activation(p_part(sig, jt), in_shares(neg_p[jt]), ACT.Sigmoid)
+            nc.scalar.activation(p_part(sig, jt), in_shares(neg_p[jt]), ACT.Sigmoid, scale=side[:, jt:jt + 1])
 
         mean = [psum.tile([P, S], F32, name=f"mean{mt}", tag=f"m{mt}") for mt in range(MT)]
         for o in range(PASSES):
-            quantise("m", o, 1.0)
+            round_weights("m", o, 1.0)
+            quantise("m", o)
             for mt in range(MT):
                 cols = slice(mt * P, (mt + 1) * P)
                 nc.tensor.matmul_mx(out=mean[mt][:], lhsT=codes["m", o][:, cols].bitcast(FP8X4), lhsT_scale=planes["m", o][:, cols],
                                     rhs=x_codes[o][:].bitcast(FP8X4), rhs_scale=x_planes[4 * o:P, :],
                                     start=(o == 0), stop=(o == PASSES - 1))
-
-        sg_scale = keep.tile([P, JT], F32, name="sg_scale")
-        sg_bias = keep.tile([P, JT], F32, name="sg_bias")
-        nc.gpsimd.tensor_scalar(sg_scale[:], bought[:], -0.7, 0.0, ALU.mult, ALU.add)
-        nc.gpsimd.tensor_scalar(sg_bias[:], bought[:], -1.0, 1.0, ALU.mult, ALU.add)
 
         miss = keep.tile([P, MT, S], F32, name="miss")
         miss_sq = keep.tile([P, MT, S], F32, name="miss_sq")
@@ -140,18 +150,18 @@ def tile_picked_yziln_nll_p_kernel(tc, x_words, x_scales, w1, w2, w3, buys, logv
             nc.vector.tensor_tensor(miss[:, mt, :], mean[mt][:], spent[:, mt, :], ALU.subtract)
 
         logsig = keep.tile([P, JT, 2 * N], F32, name="logsig")
-        soft = keep.tile([P, 2, JT, N], F32, name="soft")
+        soft = keep.tile([P, JT, N], F32, name="soft")
         cut = N + share // 2
         for h in range(2):
             rows = slice(2 * h, 2 * h + 2)
-            nc.scalar.activation(logsig[:, rows, 0:cut], sig[:, rows, 0:cut], ACT.Ln, bias=FLOOR, scale=math.exp(-SHIFT))
+            nc.scalar.activation(logsig[:, rows, 0:cut], sig[:, rows, 0:cut], ACT.Ln, bias=FLOOR)
             for jt in range(2 * h, 2 * h + 2):
-                nc.vector.scalar_tensor_tensor(soft[:, 0, jt, :], neg_s[jt], SHIFT, logsig[:, jt, 0:N], ALU.subtract, ALU.min)
-        nc.scalar.activation(logsig[:, :, cut:2 * N], sig[:, :, cut:2 * N], ACT.Ln, bias=FLOOR, scale=math.exp(-SHIFT))
+                nc.vector.tensor_tensor(soft[:, jt, :], neg_s[jt], logsig[:, jt, 0:N], ALU.min)
+        nc.scalar.activation(logsig[:, :, cut:2 * N], sig[:, :, cut:2 * N], ACT.Ln, bias=FLOOR)
 
         log_sg = keep.tile([P, JT, N], F32, name="log_sg")
         for jt in range(JT):
-            nc.scalar.activation(log_sg[:, jt, :], soft[:, 0, jt, :], ACT.Ln, bias=sg_bias[:, jt:jt + 1], scale=sg_scale[:, jt:jt + 1])
+            nc.scalar.activation(log_sg[:, jt, :], soft[:, jt, :], ACT.Ln, bias=sg_bias[:, jt:jt + 1], scale=sg_scale[:, jt:jt + 1])
 
         for mt in range(MT):
             nc.gpsimd.tensor_tensor(miss_sq[:, mt, :], miss[:, mt, :], miss[:, mt, :], ALU.mult)
@@ -162,38 +172,50 @@ def tile_picked_yziln_nll_p_kernel(tc, x_words, x_scales, w1, w2, w3, buys, logv
 
         odds = keep.tile([P, JT, N], F32, name="odds")
         for jt in range(JT):
-            nc.vector.scalar_tensor_tensor(in_shares(soft[:, 1, jt, :]), in_shares(neg_p[jt]), SHIFT, p_part(logsig, jt), ALU.subtract, ALU.min)
-        for jt in range(JT):
-            nc.vector.scalar_tensor_tensor(odds[:, jt, :], neg_p[jt], bought[:, jt:jt + 1], soft[:, 1, jt, :], ALU.mult, ALU.subtract)
+            nc.vector.scalar_tensor_tensor(in_shares(odds[:, jt, :]), in_shares(neg_p[jt]), side[:, jt:jt + 1], p_part(logsig, jt), ALU.mult, ALU.min)
+        neg_log_sg = keep.tile([P, JT, N], F32, name="neg_log_sg")
+        for h in range(2):
+            nc.vector.tensor_scalar(neg_log_sg[:, 2 * h:2 * h + 2, :], log_sg[:, 2 * h:2 * h + 2, :], -1.0, None, ALU.mult)
 
-        total = [[psum.tile([P, 2, P], F32, name=f"total{h}{mt}", tag=f"b{2 + 2 * h + mt}") for mt in range(MT)] for h in range(2)]
+        total_early = [psum.tile([P, 2, P], F32, name=f"total_early{mt}", tag=f"b{2 + mt}") for mt in range(MT)]
+        total_third = psum.tile([P, MT, P], F32, name="total_third", tag="b4")
+        total_last = [psum.tile([P, P], F32, name=f"total_last{mt}", tag=("b5", "b0")[mt]) for mt in range(MT)]
 
         def add_turned(term, jt, mt, first, last):
-            nc.tensor.matmul(total[jt // 2][mt][:, jt % 2, :], term[:, jt, mt * P:(mt + 1) * P], identity[:],
-                             is_transpose=True, start=first and jt % 2 == 0, stop=last and jt % 2 == 1)
+            if jt < 2:
+                dst, opens, closes = total_early[mt][:, jt, :], jt == 0, jt == 1
+            elif jt == 2:
+                dst, opens, closes = total_third[:, mt, :], mt == 0, mt == 1
+            else:
+                dst, opens, closes = total_last[mt][:], True, True
+            nc.tensor.matmul(dst, term[:, jt, mt * P:(mt + 1) * P], identity[:], is_transpose=True, start=first and opens, stop=last and closes)
 
-        for term in (log_sg, odds):
+        for term in (odds, neg_log_sg):
             for jt in range(JT):
                 for mt in range(MT):
-                    add_turned(term, jt, mt, term is log_sg, False)
+                    add_turned(term, jt, mt, term is odds, False)
 
         inv_var = keep.tile([P, JT, N], F32, name="inv_var")
         fit = keep.tile([P, JT, N], F32, name="fit")
-        fit_bias = keep.tile([P, JT], F32, name="fit_bias")
-        nc.gpsimd.tensor_scalar(fit_bias[:], sg_bias[:], -200.0, math.log(0.5), ALU.mult, ALU.add)
-        for jt in range(JT):
-            nc.scalar.activation(inv_var[:, jt, :], log_sg[:, jt, :], ACT.Exp, scale=-2.0, bias=fit_bias[:, jt:jt + 1])
-        for jt in range(JT):
-            nc.vector.tensor_tensor(fit[:, jt, :], miss_sq_t[jt // 2][:, jt % 2, :], inv_var[:, jt, :], ALU.mult)
-            for mt in range(MT):
+        pieces = [(jt, range(MT)) for jt in range(JT - 1)] + [(JT - 1, range(mt, mt + 1)) for mt in range(MT)]
+        for jt, mts in pieces:
+            cols = slice(mts[0] * P, (mts[-1] + 1) * P)
+            nc.scalar.activation(inv_var[:, jt, cols], log_sg[:, jt, cols], ACT.Exp, scale=-2.0, bias=fit_bias[:, jt:jt + 1])
+        for jt, mts in pieces:
+            cols = slice(mts[0] * P, (mts[-1] + 1) * P)
+            nc.vector.scalar_tensor_tensor(fit[:, jt, cols], miss_sq_t[jt // 2][:, jt % 2, cols], -0.5, inv_var[:, jt, cols], ALU.mult, ALU.mult)
+            for mt in mts:
                 add_turned(fit, jt, mt, False, True)
         out_view = out.rearrange("(t p) j -> p t j", p=P)
         early = keep.tile([P, MT, 2 * P], F32, name="early")
         for mt in range(MT):
-            nc.scalar.activation(early[:, mt, :], total[0][mt][:].rearrange("p a b -> p (a b)"), ACT.Copy, bias=-SHIFT)
+            nc.scalar.activation(early[:, mt, :], total_early[mt][:].rearrange("p a b -> p (a b)"), ACT.Copy, scale=-1.0)
         nc.sync.dma_start(out_view[:, :, 0:2 * P], early[:])
-        late = [keep.tile([P, 2 * P], F32, name=f"late{mt}") for mt in range(MT)]
-        nc.scalar.activation(late[0][:], total[1][0][:].rearrange("p a b -> p (a b)"), ACT.Copy, bias=-SHIFT)
-        nc.scalar.dma_start(out_view[:, 0, 2 * P:S], late[0][:])
-        nc.vector.tensor_scalar(late[1][:], total[1][1][:].rearrange("p a b -> p (a b)"), SHIFT, None, ALU.subtract)
-        nc.sync.dma_start(out_view[:, 1, 2 * P:S], late[1][:])
+        third = keep.tile([P, MT, P], F32, name="third")
+        nc.vector.tensor_scalar(third[:], total_third[:], -1.0, None, ALU.mult)
+        nc.sync.dma_start(out_view[:, :, 2 * P:3 * P], third[:])
+        last = [keep.tile([P, P], F32, name=f"last{mt}") for mt in range(MT)]
+        nc.scalar.activation(last[0][:], total_last[0][:], ACT.Copy, scale=-1.0)
+        nc.scalar.dma_start(out_view[:, 0, 3 * P:S], last[0][:])
+        nc.vector.tensor_scalar(last[1][:], total_last[1][:], -1.0, None, ALU.mult)
+        nc.sync.dma_start(out_view[:, 1, 3 * P:S], last[1][:])

@@ -47,7 +47,6 @@ def tile_picked_yziln_nll_p_kernel(tc, x_words, x_scales, w1, w2, w3, buys, logv
         nc.sync.dma_start(offsets[:], offs)
         for q in range(4):
             nc.sync.dma_start(scale_table[32 * q:32 * q + 8, :].bitcast(I32), x_scales[:, 4 * q:4 * q + 4, :].bitcast(I32))
-        nc.gpsimd.dma_start(flag_rows[0:JT, :], buys[0].rearrange("(t p) -> t p", p=P))
         nc.scalar.activation(warm_out[:], warm[:], ACT.Sigmoid)
         raw = {}
 
@@ -57,6 +56,7 @@ def tile_picked_yziln_nll_p_kernel(tc, x_words, x_scales, w1, w2, w3, buys, logv
 
         load_weights("s", w3, 0)
         load_words(1)
+        nc.sync.dma_start(flag_rows[0:JT, :], buys[0].rearrange("(t p) -> t p", p=P))
         load_weights("s", w3, 1)
         for name, w in (("p", w1), ("m", w2)):
             for o in range(PASSES):
@@ -66,18 +66,18 @@ def tile_picked_yziln_nll_p_kernel(tc, x_words, x_scales, w1, w2, w3, buys, logv
 
         identity = keep.tile([P, P], F32, name="identity")
         make_identity(nc, identity[:])
-        bought = keep.tile([P, JT], F32, name="bought")
         flags_turned = psum.tile([P, P], F32, name="flags_turned", tag="m0")
         nc.tensor.transpose(flags_turned[:], flag_rows[:], identity[:])
-        nc.scalar.copy(bought[:], flags_turned[:, 0:JT])
-        sg_scale = keep.tile([P, JT], F32, name="sg_scale")
-        sg_bias = keep.tile([P, JT], F32, name="sg_bias")
-        nc.gpsimd.tensor_scalar(sg_scale[:], bought[:], -0.7, 0.0, ALU.mult, ALU.add)
-        nc.gpsimd.tensor_scalar(sg_bias[:], bought[:], -0.7, 1.0, ALU.mult, ALU.add)
-        side = keep.tile([P, JT], F32, name="side")
-        nc.gpsimd.tensor_scalar(side[:], bought[:], -2.0, 1.0, ALU.mult, ALU.add)
-        fit_bias = keep.tile([P, JT], F32, name="fit_bias")
-        nc.gpsimd.tensor_scalar(fit_bias[:], bought[:], -1.0, 200.0, ALU.add, ALU.mult)
+
+        def from_flags(name, scale, bias):
+            column = keep.tile([P, JT], F32, name=name)
+            nc.scalar.activation(column[:], flags_turned[:, 0:JT], ACT.Copy, scale=scale, bias=bias)
+            return column
+
+        side = from_flags("side", -2.0, 1.0)
+        sg_scale = from_flags("sg_scale", -0.7, 0.0)
+        sg_bias = from_flags("sg_bias", -0.7, 1.0)
+        fit_bias = from_flags("fit_bias", 200.0, -200.0)
 
         x_planes = keep.tile([P, S], U8, name="x_planes", align_bytes=64)
         x_codes = [keep.tile([P, S], U32, name=f"x_codes{o}", align_bytes=64) for o in range(PASSES)]
@@ -164,7 +164,7 @@ def tile_picked_yziln_nll_p_kernel(tc, x_words, x_scales, w1, w2, w3, buys, logv
             nc.scalar.activation(log_sg[:, jt, :], soft[:, jt, :], ACT.Ln, bias=sg_bias[:, jt:jt + 1], scale=sg_scale[:, jt:jt + 1])
 
         for mt in range(MT):
-            nc.gpsimd.tensor_tensor(miss_sq[:, mt, :], miss[:, mt, :], miss[:, mt, :], ALU.mult)
+            nc.vector.tensor_tensor(miss_sq[:, mt, :], miss[:, mt, :], miss[:, mt, :], ALU.mult)
         miss_sq_t = [psum.tile([P, 2, N], F32, name=f"miss_sq_t{h}", tag=f"m{h}") for h in range(2)]
         for jt in range(JT):
             for mt in range(MT):
@@ -177,18 +177,11 @@ def tile_picked_yziln_nll_p_kernel(tc, x_words, x_scales, w1, w2, w3, buys, logv
         for h in range(2):
             nc.vector.tensor_scalar(neg_log_sg[:, 2 * h:2 * h + 2, :], log_sg[:, 2 * h:2 * h + 2, :], -1.0, None, ALU.mult)
 
-        total_early = [psum.tile([P, 2, P], F32, name=f"total_early{mt}", tag=f"b{2 + mt}") for mt in range(MT)]
-        total_third = psum.tile([P, MT, P], F32, name="total_third", tag="b4")
-        total_last = [psum.tile([P, P], F32, name=f"total_last{mt}", tag=("b5", "b0")[mt]) for mt in range(MT)]
+        total = [[psum.tile([P, 2, P], F32, name=f"total{h}{mt}", tag=f"b{2 + 2 * h + mt}") for mt in range(MT)] for h in range(2)]
 
         def add_turned(term, jt, mt, first, last):
-            if jt < 2:
-                dst, opens, closes = total_early[mt][:, jt, :], jt == 0, jt == 1
-            elif jt == 2:
-                dst, opens, closes = total_third[:, mt, :], mt == 0, mt == 1
-            else:
-                dst, opens, closes = total_last[mt][:], True, True
-            nc.tensor.matmul(dst, term[:, jt, mt * P:(mt + 1) * P], identity[:], is_transpose=True, start=first and opens, stop=last and closes)
+            nc.tensor.matmul(total[jt // 2][mt][:, jt % 2, :], term[:, jt, mt * P:(mt + 1) * P], identity[:],
+                             is_transpose=True, start=first and jt % 2 == 0, stop=last and jt % 2 == 1)
 
         for term in (odds, neg_log_sg):
             for jt in range(JT):
@@ -197,25 +190,19 @@ def tile_picked_yziln_nll_p_kernel(tc, x_words, x_scales, w1, w2, w3, buys, logv
 
         inv_var = keep.tile([P, JT, N], F32, name="inv_var")
         fit = keep.tile([P, JT, N], F32, name="fit")
-        pieces = [(jt, range(MT)) for jt in range(JT - 1)] + [(JT - 1, range(mt, mt + 1)) for mt in range(MT)]
-        for jt, mts in pieces:
-            cols = slice(mts[0] * P, (mts[-1] + 1) * P)
-            nc.scalar.activation(inv_var[:, jt, cols], log_sg[:, jt, cols], ACT.Exp, scale=-2.0, bias=fit_bias[:, jt:jt + 1])
-        for jt, mts in pieces:
-            cols = slice(mts[0] * P, (mts[-1] + 1) * P)
-            nc.vector.scalar_tensor_tensor(fit[:, jt, cols], miss_sq_t[jt // 2][:, jt % 2, cols], -0.5, inv_var[:, jt, cols], ALU.mult, ALU.mult)
-            for mt in mts:
+        for jt in range(JT):
+            nc.scalar.activation(inv_var[:, jt, :], log_sg[:, jt, :], ACT.Exp, scale=-2.0, bias=fit_bias[:, jt:jt + 1])
+        for jt in range(JT):
+            nc.vector.scalar_tensor_tensor(fit[:, jt, :], miss_sq_t[jt // 2][:, jt % 2, :], -0.5, inv_var[:, jt, :], ALU.mult, ALU.mult)
+            for mt in range(MT):
                 add_turned(fit, jt, mt, False, True)
         out_view = out.rearrange("(t p) j -> p t j", p=P)
         early = keep.tile([P, MT, 2 * P], F32, name="early")
         for mt in range(MT):
-            nc.scalar.activation(early[:, mt, :], total_early[mt][:].rearrange("p a b -> p (a b)"), ACT.Copy, scale=-1.0)
+            nc.scalar.activation(early[:, mt, :], total[0][mt][:].rearrange("p a b -> p (a b)"), ACT.Copy, scale=-1.0)
         nc.sync.dma_start(out_view[:, :, 0:2 * P], early[:])
-        third = keep.tile([P, MT, P], F32, name="third")
-        nc.vector.tensor_scalar(third[:], total_third[:], -1.0, None, ALU.mult)
-        nc.sync.dma_start(out_view[:, :, 2 * P:3 * P], third[:])
-        last = [keep.tile([P, P], F32, name=f"last{mt}") for mt in range(MT)]
-        nc.scalar.activation(last[0][:], total_last[0][:], ACT.Copy, scale=-1.0)
-        nc.scalar.dma_start(out_view[:, 0, 3 * P:S], last[0][:])
-        nc.vector.tensor_scalar(last[1][:], total_last[1][:], -1.0, None, ALU.mult)
-        nc.sync.dma_start(out_view[:, 1, 3 * P:S], last[1][:])
+        late = [keep.tile([P, 2 * P], F32, name=f"late{mt}") for mt in range(MT)]
+        nc.scalar.activation(late[0][:], total[1][0][:].rearrange("p a b -> p (a b)"), ACT.Copy, scale=-1.0)
+        nc.scalar.dma_start(out_view[:, 0, 2 * P:S], late[0][:])
+        nc.vector.tensor_scalar(late[1][:], total[1][1][:].rearrange("p a b -> p (a b)"), -1.0, None, ALU.mult)
+        nc.sync.dma_start(out_view[:, 1, 2 * P:S], late[1][:])

@@ -18,10 +18,18 @@ ACT = mybir.ActivationFunctionType
 
 P = 128
 PACK = 4
-PASSES = K // (P * PACK)
+K_PASS = P * PACK
+PASSES = K // K_PASS
+QUADRANT = 32
+SCALE_ROWS = 4
+LINE = 4
 JT = S // P
 MT = N // P
+HALF_JT = JT // 2
+HALF_S = S // 2
+SHARE = N // JT
 FLOOR = 2.0 ** -63
+MASK = 100.0
 
 
 def tile_picked_yziln_nll_p_kernel(tc, x_words, x_scales, w1, w2, w3, buys, logv, offs, out):
@@ -32,28 +40,28 @@ def tile_picked_yziln_nll_p_kernel(tc, x_words, x_scales, w1, w2, w3, buys, logv
 
         offsets = keep.tile([P, S // 16], U16, name="offsets")
         scale_table = keep.tile([P, T], U8, name="scale_table", align_bytes=64)
-        warm = keep.tile([P, 1], F32, name="warm")
-        warm_out = keep.tile([P, 1], F32, name="warm_out")
+        zero = keep.tile([P, 1], F32, name="zero")
+        half = keep.tile([P, 1], F32, name="half")
         nc.gpsimd.memset(scale_table[:].bitcast(I32), 0)
-        nc.gpsimd.memset(warm[:], 0.0)
+        nc.gpsimd.memset(zero[:], 0.0)
         flag_rows = keep.tile([P, P], F32, name="flag_rows")
         nc.gpsimd.memset(flag_rows[:], 0.0)
         word_tables = [keep.tile([P, T], U32, name=f"word_table{o}", align_bytes=64) for o in range(PASSES)]
+        raw = {}
 
         def load_words(o):
             nc.sync.dma_start(word_tables[o][:].bitcast(I32), x_words[o].rearrange("p n t -> p (n t)").bitcast(I32))
 
-        load_words(0)
-        nc.sync.dma_start(offsets[:], offs)
-        for q in range(4):
-            nc.sync.dma_start(scale_table[32 * q:32 * q + 8, :].bitcast(I32), x_scales[:, 4 * q:4 * q + 4, :].bitcast(I32))
-        nc.scalar.activation(warm_out[:], warm[:], ACT.Sigmoid)
-        raw = {}
-
         def load_weights(name, w, o):
             raw[name, o] = keep.tile([P, PACK, N], F32, name=f"raw_{name}{o}")
-            nc.sync.dma_start(raw[name, o][:], w[512 * o:512 * (o + 1), :].rearrange("(p t) m -> p t m", t=PACK))
+            nc.sync.dma_start(raw[name, o][:], w[K_PASS * o:K_PASS * (o + 1), :].rearrange("(p t) m -> p t m", t=PACK))
 
+        load_words(0)
+        nc.sync.dma_start(offsets[:], offs)
+        for q in range(P // QUADRANT):
+            nc.sync.dma_start(scale_table[QUADRANT * q:QUADRANT * q + PASSES * SCALE_ROWS, :].bitcast(I32),
+                              x_scales[:, SCALE_ROWS * q:SCALE_ROWS * (q + 1), :].bitcast(I32))
+        nc.scalar.activation(half[:], zero[:], ACT.Sigmoid)
         load_weights("s", w3, 0)
         load_words(1)
         nc.sync.dma_start(flag_rows[0:JT, :], buys[0].rearrange("(t p) -> t p", p=P))
@@ -77,7 +85,8 @@ def tile_picked_yziln_nll_p_kernel(tc, x_words, x_scales, w1, w2, w3, buys, logv
         side = from_flags("side", -2.0, 1.0)
         sg_scale = from_flags("sg_scale", -0.7, 0.0)
         sg_bias = from_flags("sg_bias", -0.7, 1.0)
-        fit_bias = from_flags("fit_bias", 200.0, -200.0)
+        mask_bias = from_flags("mask_bias", 2 * MASK, -2 * MASK)
+        mask_term = from_flags("mask_term", -MASK, MASK)
 
         x_planes = keep.tile([P, S], U8, name="x_planes", align_bytes=64)
         x_codes = [keep.tile([P, S], U32, name=f"x_codes{o}", align_bytes=64) for o in range(PASSES)]
@@ -85,50 +94,46 @@ def tile_picked_yziln_nll_p_kernel(tc, x_words, x_scales, w1, w2, w3, buys, logv
         nc.vector.tensor_copy(x_planes[:], scale_table[:].indirect(offsets[:]))
         nc.vector.tensor_copy(x_codes[1][:], word_tables[1][:].indirect(offsets[:]))
 
-        grouped, codes, planes = {}, {}, {}
+        codes, scales = {}, {}
 
-        def round_weights(name, o, sign, on_scalar=False):
-            grouped[name, o] = keep.tile([P, N, PACK], BF16, name=f"grouped_{name}{o}", align_bytes=64)
-            dst = grouped[name, o][:].rearrange("p (c i) t -> p c t i", i=4)
-            src = raw[name, o][:].rearrange("p t (c i) -> p c t i", i=4)
+        def quantise(name, o, sign, on_scalar=False):
+            grouped = keep.tile([P, N, PACK], BF16, name=f"grouped_{name}{o}", align_bytes=64)
+            dst = grouped[:].rearrange("p (c i) t -> p c t i", i=LINE)
+            src = raw[name, o][:].rearrange("p t (c i) -> p c t i", i=LINE)
             if on_scalar:
                 nc.scalar.activation(dst, src, ACT.Copy, scale=sign)
             else:
                 nc.vector.tensor_scalar(dst, src, sign, None, ALU.mult)
-
-        def quantise(name, o):
             codes[name, o] = keep.tile([P, N], U32, name=f"codes_{name}{o}", align_bytes=64)
-            planes[name, o] = keep.tile([P, N], U8, name=f"plane_{name}{o}", align_bytes=64)
-            nc.vector.quantize_mx(out=codes[name, o][:].bitcast(FP8X4), scales=planes[name, o][:], in_=grouped[name, o][:].rearrange("p m t -> p (m t)"))
+            scales[name, o] = keep.tile([P, N], U8, name=f"scales_{name}{o}", align_bytes=64)
+            nc.vector.quantize_mx(out=codes[name, o][:].bitcast(FP8X4), scales=scales[name, o][:],
+                                  in_=grouped[:].rearrange("p m t -> p (m t)"))
 
         def product_by_customer(dst, name, jt, o):
             cols = slice(jt * P, (jt + 1) * P)
-            nc.tensor.matmul_mx(out=dst, lhsT=x_codes[o][:, cols].bitcast(FP8X4), lhsT_scale=x_planes[4 * o:P, cols],
-                                rhs=codes[name, o][:].bitcast(FP8X4), rhs_scale=planes[name, o][:],
+            nc.tensor.matmul_mx(out=dst, lhsT=x_codes[o][:, cols].bitcast(FP8X4), lhsT_scale=x_planes[SCALE_ROWS * o:P, cols],
+                                rhs=codes[name, o][:].bitcast(FP8X4), rhs_scale=scales[name, o][:],
                                 start=(o == 0), stop=(o == PASSES - 1))
 
         sig = keep.tile([P, JT, 2 * N], F32, name="sig")
-        share = N // JT
 
         def p_part(tile, jt):
-            return tile[:, :, N + (JT - 1 - jt) * share:N + (JT - jt) * share]
+            return tile[:, :, N + (JT - 1 - jt) * SHARE:N + (JT - jt) * SHARE]
 
         def in_shares(ap):
-            return ap.rearrange("p (c i) -> p c i", i=share)
+            return ap.rearrange("p (c i) -> p c i", i=SHARE)
 
-        banks = [psum.tile([P, 2, N], F32, name=f"neg{b}", tag=f"b{b}") for b in range(6)]
+        banks = [psum.tile([P, 2, N], F32, name=f"bank{b}", tag=f"b{b}") for b in range(JT + 2)]
         neg_s = [banks[jt][:, 0, :] for jt in range(JT)]
-        neg_p = [banks[4][:, 0, :], banks[5][:, 0, :], banks[0][:, 1, :], banks[1][:, 1, :]]
+        neg_p = [banks[JT][:, 0, :], banks[JT + 1][:, 0, :], banks[0][:, 1, :], banks[1][:, 1, :]]
         for o in range(PASSES):
-            round_weights("s", o, -1.0, on_scalar=True)
-            quantise("s", o)
+            quantise("s", o, -1.0, on_scalar=True)
             for jt in range(JT):
                 product_by_customer(neg_s[jt], "s", jt, o)
         for jt in range(JT):
             nc.scalar.activation(sig[:, jt, 0:N], neg_s[jt], ACT.Sigmoid)
         for o in range(PASSES):
-            round_weights("p", o, -1.0)
-            quantise("p", o)
+            quantise("p", o, -1.0)
             for jt in range(JT):
                 product_by_customer(neg_p[jt], "p", jt, o)
         for jt in range(JT):
@@ -136,73 +141,94 @@ def tile_picked_yziln_nll_p_kernel(tc, x_words, x_scales, w1, w2, w3, buys, logv
 
         mean = [psum.tile([P, S], F32, name=f"mean{mt}", tag=f"m{mt}") for mt in range(MT)]
         for o in range(PASSES):
-            round_weights("m", o, 1.0)
-            quantise("m", o)
+            quantise("m", o, 1.0)
             for mt in range(MT):
                 cols = slice(mt * P, (mt + 1) * P)
-                nc.tensor.matmul_mx(out=mean[mt][:], lhsT=codes["m", o][:, cols].bitcast(FP8X4), lhsT_scale=planes["m", o][:, cols],
-                                    rhs=x_codes[o][:].bitcast(FP8X4), rhs_scale=x_planes[4 * o:P, :],
+                nc.tensor.matmul_mx(out=mean[mt][:], lhsT=codes["m", o][:, cols].bitcast(FP8X4), lhsT_scale=scales["m", o][:, cols],
+                                    rhs=x_codes[o][:].bitcast(FP8X4), rhs_scale=x_planes[SCALE_ROWS * o:P, :],
                                     start=(o == 0), stop=(o == PASSES - 1))
-
         miss = keep.tile([P, MT, S], F32, name="miss")
-        miss_sq = keep.tile([P, MT, S], F32, name="miss_sq")
+        half_sq = keep.tile([P, MT, S], F32, name="half_sq")
         for mt in range(MT):
             nc.vector.tensor_tensor(miss[:, mt, :], mean[mt][:], spent[:, mt, :], ALU.subtract)
 
-        logsig = keep.tile([P, JT, 2 * N], F32, name="logsig")
-        soft = keep.tile([P, JT, N], F32, name="soft")
-        cut = N + share // 2
-        for h in range(2):
-            rows = slice(2 * h, 2 * h + 2)
-            nc.scalar.activation(logsig[:, rows, 0:cut], sig[:, rows, 0:cut], ACT.Ln, bias=FLOOR)
-            for jt in range(2 * h, 2 * h + 2):
-                nc.vector.tensor_tensor(soft[:, jt, :], neg_s[jt], logsig[:, jt, 0:N], ALU.min)
-        nc.scalar.activation(logsig[:, :, cut:2 * N], sig[:, :, cut:2 * N], ACT.Ln, bias=FLOOR)
+        log_sig = keep.tile([P, JT, 2 * N], F32, name="log_sig")
+        neg_soft_s = keep.tile([P, JT, N], F32, name="neg_soft_s")
+        cut = N + SHARE // 2
+        for first in range(0, JT, HALF_JT):
+            rows = slice(first, first + HALF_JT)
+            nc.scalar.activation(log_sig[:, rows, 0:cut], sig[:, rows, 0:cut], ACT.Ln, bias=FLOOR)
+            for jt in range(first, first + HALF_JT):
+                nc.vector.tensor_tensor(neg_soft_s[:, jt, :], neg_s[jt], log_sig[:, jt, 0:N], ALU.min)
+        nc.scalar.activation(log_sig[:, :, cut:2 * N], sig[:, :, cut:2 * N], ACT.Ln, bias=FLOOR)
 
         log_sg = keep.tile([P, JT, N], F32, name="log_sg")
         for jt in range(JT):
-            nc.scalar.activation(log_sg[:, jt, :], soft[:, jt, :], ACT.Ln, bias=sg_bias[:, jt:jt + 1], scale=sg_scale[:, jt:jt + 1])
+            nc.scalar.activation(log_sg[:, jt, :], neg_soft_s[:, jt, :], ACT.Ln, bias=sg_bias[:, jt:jt + 1], scale=sg_scale[:, jt:jt + 1])
 
         for mt in range(MT):
-            nc.vector.tensor_tensor(miss_sq[:, mt, :], miss[:, mt, :], miss[:, mt, :], ALU.mult)
-        miss_sq_t = [psum.tile([P, 2, N], F32, name=f"miss_sq_t{h}", tag=f"m{h}") for h in range(2)]
-        for jt in range(JT):
+            nc.vector.scalar_tensor_tensor(half_sq[:, mt, :], miss[:, mt, :], half[:], miss[:, mt, :], ALU.mult, ALU.mult)
+        half_sq_turned = psum.tile([P, HALF_JT, N], F32, name="half_sq_turned", tag="m0")
+        for jt in range(HALF_JT):
             for mt in range(MT):
-                nc.tensor.transpose(miss_sq_t[jt // 2][:, jt % 2, mt * P:(mt + 1) * P], miss_sq[:, mt, jt * P:(jt + 1) * P], identity[:])
+                nc.tensor.transpose(half_sq_turned[:, jt, mt * P:(mt + 1) * P], half_sq[:, mt, jt * P:(jt + 1) * P], identity[:])
 
-        odds = keep.tile([P, JT, N], F32, name="odds")
+        neg_soft_p = keep.tile([P, JT, N], F32, name="neg_soft_p")
         for jt in range(JT):
-            nc.vector.scalar_tensor_tensor(in_shares(odds[:, jt, :]), in_shares(neg_p[jt]), side[:, jt:jt + 1], p_part(logsig, jt), ALU.mult, ALU.min)
+            nc.vector.scalar_tensor_tensor(in_shares(neg_soft_p[:, jt, :]), in_shares(neg_p[jt]), side[:, jt:jt + 1],
+                                           p_part(log_sig, jt), ALU.mult, ALU.min)
         neg_log_sg = keep.tile([P, JT, N], F32, name="neg_log_sg")
-        for h in range(2):
-            nc.vector.tensor_scalar(neg_log_sg[:, 2 * h:2 * h + 2, :], log_sg[:, 2 * h:2 * h + 2, :], -1.0, None, ALU.mult)
+        for first in range(0, JT, HALF_JT):
+            rows = slice(first, first + HALF_JT)
+            nc.vector.tensor_scalar(neg_log_sg[:, rows, :], log_sg[:, rows, :], -1.0, None, ALU.mult)
 
-        total = [[psum.tile([P, 2, P], F32, name=f"total{h}{mt}", tag=f"b{2 + 2 * h + mt}") for mt in range(MT)] for h in range(2)]
+        neg_total = [psum.tile([P, HALF_JT, P], F32, name=f"neg_total{mt}", tag=f"b{2 + mt}") for mt in range(MT)]
+        neg_rest = psum.tile([P, MT, HALF_JT, P], F32, name="neg_rest", tag=f"b{JT}")
+        exponent = psum.tile([P, MT, HALF_JT, P], F32, name="exponent", tag=f"b{JT + 1}")
 
-        def add_turned(term, jt, mt, first, last):
-            nc.tensor.matmul(total[jt // 2][mt][:, jt % 2, :], term[:, jt, mt * P:(mt + 1) * P], identity[:],
-                             is_transpose=True, start=first and jt % 2 == 0, stop=last and jt % 2 == 1)
+        def add_turned(dst, src, start, stop):
+            nc.tensor.matmul(dst, src, identity[:], is_transpose=True, start=start, stop=stop)
 
-        for term in (odds, neg_log_sg):
-            for jt in range(JT):
-                for mt in range(MT):
-                    add_turned(term, jt, mt, term is odds, False)
+        def block(term, jt, mt):
+            return term[:, jt, mt * P:(mt + 1) * P]
 
-        inv_var = keep.tile([P, JT, N], F32, name="inv_var")
-        fit = keep.tile([P, JT, N], F32, name="fit")
-        for jt in range(JT):
-            nc.scalar.activation(inv_var[:, jt, :], log_sg[:, jt, :], ACT.Exp, scale=-2.0, bias=fit_bias[:, jt:jt + 1])
-        for jt in range(JT):
-            nc.vector.scalar_tensor_tensor(fit[:, jt, :], miss_sq_t[jt // 2][:, jt % 2, :], -0.5, inv_var[:, jt, :], ALU.mult, ALU.mult)
-            for mt in range(MT):
-                add_turned(fit, jt, mt, False, True)
-        out_view = out.rearrange("(t p) j -> p t j", p=P)
-        early = keep.tile([P, MT, 2 * P], F32, name="early")
+        first_blocks = [(jt, mt) for jt in range(HALF_JT) for mt in range(MT)]
+        second_blocks = [(jt, mt) for jt in range(HALF_JT, JT) for mt in range(MT)]
+        for jt, mt in second_blocks:
+            add_turned(exponent[:, mt, jt - HALF_JT, :], mask_term[:, jt:jt + 1].to_broadcast([P, P]), (jt, mt) == second_blocks[0], False)
+        for jt, mt in first_blocks:
+            add_turned(neg_total[mt][:, jt, :], block(neg_soft_p, jt, mt), jt == 0, False)
+        for jt, mt in second_blocks:
+            add_turned(neg_rest[:, mt, jt - HALF_JT, :], block(neg_soft_p, jt, mt), (jt, mt) == second_blocks[0], False)
+        for jt, mt in second_blocks:
+            add_turned(exponent[:, mt, jt - HALF_JT, :], block(log_sg, jt, mt), False, (jt, mt) == second_blocks[-1])
+        for jt, mt in first_blocks:
+            add_turned(neg_total[mt][:, jt, :], block(neg_log_sg, jt, mt), False, False)
+        for jt, mt in second_blocks:
+            add_turned(neg_rest[:, mt, jt - HALF_JT, :], block(neg_log_sg, jt, mt), False, (jt, mt) == second_blocks[-1])
+
+        inv_var_first = keep.tile([P, HALF_JT, N], F32, name="inv_var_first")
+        inv_var_second = keep.tile([P, MT, HALF_S], F32, name="inv_var_second")
+        neg_fit_first = keep.tile([P, HALF_JT, N], F32, name="neg_fit_first")
+        fit_second = keep.tile([P, MT, HALF_S], F32, name="fit_second")
+        for jt in range(HALF_JT):
+            nc.scalar.activation(inv_var_first[:, jt, :], log_sg[:, jt, :], ACT.Exp, scale=-2.0, bias=mask_bias[:, jt:jt + 1])
         for mt in range(MT):
-            nc.scalar.activation(early[:, mt, :], total[0][mt][:].rearrange("p a b -> p (a b)"), ACT.Copy, scale=-1.0)
-        nc.sync.dma_start(out_view[:, :, 0:2 * P], early[:])
-        late = [keep.tile([P, 2 * P], F32, name=f"late{mt}") for mt in range(MT)]
-        nc.scalar.activation(late[0][:], total[1][0][:].rearrange("p a b -> p (a b)"), ACT.Copy, scale=-1.0)
-        nc.scalar.dma_start(out_view[:, 0, 2 * P:S], late[0][:])
-        nc.vector.tensor_scalar(late[1][:], total[1][1][:].rearrange("p a b -> p (a b)"), -1.0, None, ALU.mult)
-        nc.sync.dma_start(out_view[:, 1, 2 * P:S], late[1][:])
+            nc.scalar.activation(inv_var_second[:, mt, :], exponent[:, mt].rearrange("p a b -> p (a b)"), ACT.Exp, scale=-2.0)
+        for jt in range(HALF_JT):
+            nc.vector.scalar_tensor_tensor(neg_fit_first[:, jt, :], half_sq_turned[:, jt, :], -1.0, inv_var_first[:, jt, :], ALU.mult, ALU.mult)
+            for mt in range(MT):
+                add_turned(neg_total[mt][:, jt, :], block(neg_fit_first, jt, mt), False, jt == HALF_JT - 1)
+        for mt in range(MT):
+            nc.vector.tensor_tensor(fit_second[:, mt, :], half_sq[:, mt, HALF_S:S], inv_var_second[:, mt, :], ALU.mult)
+
+        out_tiles = out.rearrange("(t p) j -> p t j", p=P)
+        for mt in range(MT):
+            result = keep.tile([P, HALF_S], F32, name=f"result_second{mt}")
+            nc.vector.tensor_tensor(result[:], fit_second[:, mt, :], neg_rest[:, mt].rearrange("p a b -> p (a b)"), ALU.subtract)
+            nc.sync.dma_start(out_tiles[:, mt, HALF_S:S], result[:])
+        results = [keep.tile([P, HALF_S], F32, name=f"result_first{mt}") for mt in range(MT)]
+        for mt in range(MT):
+            nc.scalar.activation(results[mt][:], neg_total[mt][:].rearrange("p a b -> p (a b)"), ACT.Copy, scale=-1.0)
+        for mt in range(MT):
+            nc.scalar.dma_start(out_tiles[:, mt, 0:HALF_S], results[mt][:])

from contextlib import ExitStack

import concourse.mybir as mybir
from concourse.masks import make_identity

K, T, S, N = 1024, 1024, 512, 256
FLOPS = 3 * 2 * K * S * N

F32 = mybir.dt.float32
BF16 = mybir.dt.bfloat16
I32 = mybir.dt.int32
U32 = mybir.dt.uint32
U16 = mybir.dt.uint16
U8 = mybir.dt.uint8
FP8X4 = mybir.dt.float8_e4m3fn_x4
ALU = mybir.AluOpType
ACT = mybir.ActivationFunctionType

P = 128
PACK = 4
K_PASS = P * PACK
PASSES = K // K_PASS
QUADRANT = 32
SCALE_ROWS = 4
LINE = 4
JT = S // P
MT = N // P
HALF_JT = JT // 2
HALF_S = S // 2
SHARE = N // JT
FLOOR = 2.0 ** -63
MASK = 100.0


def tile_picked_yziln_nll_p_kernel(tc, x_words, x_scales, w1, w2, w3, buys, logv, offs, out):
    nc = tc.nc
    with ExitStack() as ctx:
        keep = ctx.enter_context(tc.tile_pool(name="keep", bufs=1))
        psum = ctx.enter_context(tc.psum_pool(name="psum", bufs=1))

        offsets = keep.tile([P, S // 16], U16, name="offsets")
        scale_table = keep.tile([P, T], U8, name="scale_table", align_bytes=64)
        zero = keep.tile([P, 1], F32, name="zero")
        half = keep.tile([P, 1], F32, name="half")
        nc.gpsimd.memset(scale_table[:].bitcast(I32), 0)
        nc.gpsimd.memset(zero[:], 0.0)
        flag_rows = keep.tile([P, P], F32, name="flag_rows")
        nc.gpsimd.memset(flag_rows[:], 0.0)
        word_tables = [keep.tile([P, T], U32, name=f"word_table{o}", align_bytes=64) for o in range(PASSES)]
        raw = {}

        def load_words(o):
            nc.sync.dma_start(word_tables[o][:].bitcast(I32), x_words[o].rearrange("p n t -> p (n t)").bitcast(I32))

        def load_weights(name, w, o):
            raw[name, o] = keep.tile([P, PACK, N], F32, name=f"raw_{name}{o}")
            nc.sync.dma_start(raw[name, o][:], w[K_PASS * o:K_PASS * (o + 1), :].rearrange("(p t) m -> p t m", t=PACK))

        load_words(0)
        nc.sync.dma_start(offsets[:], offs)
        for q in range(P // QUADRANT):
            nc.sync.dma_start(scale_table[QUADRANT * q:QUADRANT * q + PASSES * SCALE_ROWS, :].bitcast(I32),
                              x_scales[:, SCALE_ROWS * q:SCALE_ROWS * (q + 1), :].bitcast(I32))
        nc.scalar.activation(half[:], zero[:], ACT.Sigmoid)
        load_weights("s", w3, 0)
        load_words(1)
        nc.sync.dma_start(flag_rows[0:JT, :], buys[0].rearrange("(t p) -> t p", p=P))
        load_weights("s", w3, 1)
        for name, w in (("p", w1), ("m", w2)):
            for o in range(PASSES):
                load_weights(name, w, o)
        spent = keep.tile([P, MT, S], F32, name="spent")
        nc.sync.dma_start(spent[:], logv.rearrange("(t p) j -> p t j", p=P))

        identity = keep.tile([P, P], F32, name="identity")
        make_identity(nc, identity[:])
        flags_turned = psum.tile([P, P], F32, name="flags_turned", tag="m0")
        nc.tensor.transpose(flags_turned[:], flag_rows[:], identity[:])

        def from_flags(name, scale, bias):
            column = keep.tile([P, JT], F32, name=name)
            nc.scalar.activation(column[:], flags_turned[:, 0:JT], ACT.Copy, scale=scale, bias=bias)
            return column

        side = from_flags("side", -2.0, 1.0)
        sg_scale = from_flags("sg_scale", -0.7, 0.0)
        sg_bias = from_flags("sg_bias", -0.7, 1.0)
        mask_bias = from_flags("mask_bias", 2 * MASK, -2 * MASK)
        mask_term = from_flags("mask_term", -MASK, MASK)

        x_planes = keep.tile([P, S], U8, name="x_planes", align_bytes=64)
        x_codes = [keep.tile([P, S], U32, name=f"x_codes{o}", align_bytes=64) for o in range(PASSES)]
        nc.vector.tensor_copy(x_codes[0][:], word_tables[0][:].indirect(offsets[:]))
        nc.vector.tensor_copy(x_planes[:], scale_table[:].indirect(offsets[:]))
        nc.vector.tensor_copy(x_codes[1][:], word_tables[1][:].indirect(offsets[:]))

        codes, scales = {}, {}

        def quantise(name, o, sign, on_scalar=False):
            grouped = keep.tile([P, N, PACK], BF16, name=f"grouped_{name}{o}", align_bytes=64)
            dst = grouped[:].rearrange("p (c i) t -> p c t i", i=LINE)
            src = raw[name, o][:].rearrange("p t (c i) -> p c t i", i=LINE)
            if on_scalar:
                nc.scalar.activation(dst, src, ACT.Copy, scale=sign)
            else:
                nc.vector.tensor_scalar(dst, src, sign, None, ALU.mult)
            codes[name, o] = keep.tile([P, N], U32, name=f"codes_{name}{o}", align_bytes=64)
            scales[name, o] = keep.tile([P, N], U8, name=f"scales_{name}{o}", align_bytes=64)
            nc.vector.quantize_mx(out=codes[name, o][:].bitcast(FP8X4), scales=scales[name, o][:],
                                  in_=grouped[:].rearrange("p m t -> p (m t)"))

        def product_by_customer(dst, name, jt, o):
            cols = slice(jt * P, (jt + 1) * P)
            nc.tensor.matmul_mx(out=dst, lhsT=x_codes[o][:, cols].bitcast(FP8X4), lhsT_scale=x_planes[SCALE_ROWS * o:P, cols],
                                rhs=codes[name, o][:].bitcast(FP8X4), rhs_scale=scales[name, o][:],
                                start=(o == 0), stop=(o == PASSES - 1))

        sig = keep.tile([P, JT, 2 * N], F32, name="sig")

        def p_part(tile, jt):
            return tile[:, :, N + (JT - 1 - jt) * SHARE:N + (JT - jt) * SHARE]

        def in_shares(ap):
            return ap.rearrange("p (c i) -> p c i", i=SHARE)

        banks = [psum.tile([P, 2, N], F32, name=f"bank{b}", tag=f"b{b}") for b in range(JT + 2)]
        neg_s = [banks[jt][:, 0, :] for jt in range(JT)]
        neg_p = [banks[JT][:, 0, :], banks[JT + 1][:, 0, :], banks[0][:, 1, :], banks[1][:, 1, :]]
        for o in range(PASSES):
            quantise("s", o, -1.0, on_scalar=True)
            for jt in range(JT):
                product_by_customer(neg_s[jt], "s", jt, o)
        for jt in range(JT):
            nc.scalar.activation(sig[:, jt, 0:N], neg_s[jt], ACT.Sigmoid)
        for o in range(PASSES):
            quantise("p", o, -1.0)
            for jt in range(JT):
                product_by_customer(neg_p[jt], "p", jt, o)
        for jt in range(JT):
            nc.scalar.activation(p_part(sig, jt), in_shares(neg_p[jt]), ACT.Sigmoid, scale=side[:, jt:jt + 1])

        mean = [psum.tile([P, S], F32, name=f"mean{mt}", tag=f"m{mt}") for mt in range(MT)]
        for o in range(PASSES):
            quantise("m", o, 1.0)
            for mt in range(MT):
                cols = slice(mt * P, (mt + 1) * P)
                nc.tensor.matmul_mx(out=mean[mt][:], lhsT=codes["m", o][:, cols].bitcast(FP8X4), lhsT_scale=scales["m", o][:, cols],
                                    rhs=x_codes[o][:].bitcast(FP8X4), rhs_scale=x_planes[SCALE_ROWS * o:P, :],
                                    start=(o == 0), stop=(o == PASSES - 1))
        miss = keep.tile([P, MT, S], F32, name="miss")
        half_sq = keep.tile([P, MT, S], F32, name="half_sq")
        for mt in range(MT):
            nc.vector.tensor_tensor(miss[:, mt, :], mean[mt][:], spent[:, mt, :], ALU.subtract)

        log_sig = keep.tile([P, JT, 2 * N], F32, name="log_sig")
        neg_soft_s = keep.tile([P, JT, N], F32, name="neg_soft_s")
        cut = N + SHARE // 2
        for first in range(0, JT, HALF_JT):
            rows = slice(first, first + HALF_JT)
            nc.scalar.activation(log_sig[:, rows, 0:cut], sig[:, rows, 0:cut], ACT.Ln, bias=FLOOR)
            for jt in range(first, first + HALF_JT):
                nc.vector.tensor_tensor(neg_soft_s[:, jt, :], neg_s[jt], log_sig[:, jt, 0:N], ALU.min)
        nc.scalar.activation(log_sig[:, :, cut:2 * N], sig[:, :, cut:2 * N], ACT.Ln, bias=FLOOR)

        log_sg = keep.tile([P, JT, N], F32, name="log_sg")
        for jt in range(JT):
            nc.scalar.activation(log_sg[:, jt, :], neg_soft_s[:, jt, :], ACT.Ln, bias=sg_bias[:, jt:jt + 1], scale=sg_scale[:, jt:jt + 1])

        for mt in range(MT):
            nc.vector.scalar_tensor_tensor(half_sq[:, mt, :], miss[:, mt, :], half[:], miss[:, mt, :], ALU.mult, ALU.mult)
        half_sq_turned = psum.tile([P, HALF_JT, N], F32, name="half_sq_turned", tag="m0")
        for jt in range(HALF_JT):
            for mt in range(MT):
                nc.tensor.transpose(half_sq_turned[:, jt, mt * P:(mt + 1) * P], half_sq[:, mt, jt * P:(jt + 1) * P], identity[:])

        neg_soft_p = keep.tile([P, JT, N], F32, name="neg_soft_p")
        for jt in range(JT):
            nc.vector.scalar_tensor_tensor(in_shares(neg_soft_p[:, jt, :]), in_shares(neg_p[jt]), side[:, jt:jt + 1],
                                           p_part(log_sig, jt), ALU.mult, ALU.min)
        neg_log_sg = keep.tile([P, JT, N], F32, name="neg_log_sg")
        for first in range(0, JT, HALF_JT):
            rows = slice(first, first + HALF_JT)
            nc.vector.tensor_scalar(neg_log_sg[:, rows, :], log_sg[:, rows, :], -1.0, None, ALU.mult)

        neg_total = [psum.tile([P, HALF_JT, P], F32, name=f"neg_total{mt}", tag=f"b{2 + mt}") for mt in range(MT)]
        neg_rest = psum.tile([P, MT, HALF_JT, P], F32, name="neg_rest", tag=f"b{JT}")
        exponent = psum.tile([P, MT, HALF_JT, P], F32, name="exponent", tag=f"b{JT + 1}")

        def add_turned(dst, src, start, stop):
            nc.tensor.matmul(dst, src, identity[:], is_transpose=True, start=start, stop=stop)

        def block(term, jt, mt):
            return term[:, jt, mt * P:(mt + 1) * P]

        first_blocks = [(jt, mt) for jt in range(HALF_JT) for mt in range(MT)]
        second_blocks = [(jt, mt) for jt in range(HALF_JT, JT) for mt in range(MT)]
        for jt, mt in second_blocks:
            add_turned(exponent[:, mt, jt - HALF_JT, :], mask_term[:, jt:jt + 1].to_broadcast([P, P]), (jt, mt) == second_blocks[0], False)
        for jt, mt in first_blocks:
            add_turned(neg_total[mt][:, jt, :], block(neg_soft_p, jt, mt), jt == 0, False)
        for jt, mt in second_blocks:
            add_turned(neg_rest[:, mt, jt - HALF_JT, :], block(neg_soft_p, jt, mt), (jt, mt) == second_blocks[0], False)
        for jt, mt in second_blocks:
            add_turned(exponent[:, mt, jt - HALF_JT, :], block(log_sg, jt, mt), False, (jt, mt) == second_blocks[-1])
        for jt, mt in first_blocks:
            add_turned(neg_total[mt][:, jt, :], block(neg_log_sg, jt, mt), False, False)
        for jt, mt in second_blocks:
            add_turned(neg_rest[:, mt, jt - HALF_JT, :], block(neg_log_sg, jt, mt), False, (jt, mt) == second_blocks[-1])

        inv_var_first = keep.tile([P, HALF_JT, N], F32, name="inv_var_first")
        inv_var_second = keep.tile([P, MT, HALF_S], F32, name="inv_var_second")
        neg_fit_first = keep.tile([P, HALF_JT, N], F32, name="neg_fit_first")
        fit_second = keep.tile([P, MT, HALF_S], F32, name="fit_second")
        for jt in range(HALF_JT):
            nc.scalar.activation(inv_var_first[:, jt, :], log_sg[:, jt, :], ACT.Exp, scale=-2.0, bias=mask_bias[:, jt:jt + 1])
        for mt in range(MT):
            nc.scalar.activation(inv_var_second[:, mt, :], exponent[:, mt].rearrange("p a b -> p (a b)"), ACT.Exp, scale=-2.0)
        for jt in range(HALF_JT):
            nc.vector.scalar_tensor_tensor(neg_fit_first[:, jt, :], half_sq_turned[:, jt, :], -1.0, inv_var_first[:, jt, :], ALU.mult, ALU.mult)
            for mt in range(MT):
                add_turned(neg_total[mt][:, jt, :], block(neg_fit_first, jt, mt), False, jt == HALF_JT - 1)
        for mt in range(MT):
            nc.vector.tensor_tensor(fit_second[:, mt, :], half_sq[:, mt, HALF_S:S], inv_var_second[:, mt, :], ALU.mult)

        out_tiles = out.rearrange("(t p) j -> p t j", p=P)
        for mt in range(MT):
            result = keep.tile([P, HALF_S], F32, name=f"result_second{mt}")
            nc.vector.tensor_tensor(result[:], fit_second[:, mt, :], neg_rest[:, mt].rearrange("p a b -> p (a b)"), ALU.subtract)
            nc.sync.dma_start(out_tiles[:, mt, HALF_S:S], result[:])
        results = [keep.tile([P, HALF_S], F32, name=f"result_first{mt}") for mt in range(MT)]
        for mt in range(MT):
            nc.scalar.activation(results[mt][:], neg_total[mt][:].rearrange("p a b -> p (a b)"), ACT.Copy, scale=-1.0)
        for mt in range(MT):
            nc.scalar.dma_start(out_tiles[:, mt, 0:HALF_S], results[mt][:])
